import numpy as np
import ml_dtypes


def mxq(x, axis, fmt="e4m3"):
    dtype, down = {"e4m3": (ml_dtypes.float8_e4m3fn, 7), "e5m2": (ml_dtypes.float8_e5m2, 14)}[fmt]
    v = np.moveaxis(np.asarray(x, np.float32).astype(ml_dtypes.bfloat16).astype(np.float64), axis, -1)
    blocks = v.reshape(v.shape[:-1] + (-1, 32))
    amax = np.abs(blocks).max(-1, keepdims=True)
    byte = np.maximum(np.where(amax > 0, np.frexp(amax)[1] - 1 + 127, 0) - down, 1)
    scale = np.exp2(byte - 127.0)
    codes = (blocks / scale).astype(np.float32).astype(dtype).astype(np.float64)
    return np.moveaxis((codes * scale).reshape(v.shape), -1, axis)


WIDE = False


def mx_kscale(k):
    if not WIDE:
        return np.ones(k)
    levels = np.array([10, -10, 5, -5, 0])
    if k % 512:
        return np.exp2(np.random.permutation(np.resize(levels, k // 32))).repeat(32)
    a = np.empty((k // 512, 16))
    for p in range(k // 512):
        a[p, :8] = np.random.permutation(np.resize(levels, 8))
        for g in range(8):
            far = levels[np.abs(levels - a[p, g]) >= 10]
            a[p, g + 8] = far[np.random.randint(len(far))]
    return np.exp2(a.ravel()).repeat(32)


def f64(x):
    return np.asarray(x).astype(np.float64)


def striped(idx):
    return np.tile(idx.reshape(-1, 16).T, (8, 1)).astype(np.uint16)


def unstriped(offs):
    return offs[:16].T.reshape(-1).astype(np.int64)


def striped8(idx):
    return np.concatenate([x.reshape(-1, 16).T for x in idx]).astype(np.uint16)


def runs(offs, k):
    lists = np.stack([offs[16 * r : 16 * r + 16].T.reshape(-1) for r in range(8)]).astype(np.int64)
    return lists[np.arange(k) % 512 // 64]


def pack_weight(w):
    k, n = w.shape
    w = f64(np.asarray(w, np.float32).astype(ml_dtypes.bfloat16)).reshape(k // 32, 32, n)
    amax = np.abs(w).max(1)
    byte = np.clip(np.where(amax > 0, np.frexp(amax)[1] - 1 + 127 - 7, 1), 1, 254)
    scaled = (w * np.exp2(127.0 - byte)[:, None, :]).reshape(k, n).astype(np.float32)
    words = np.ascontiguousarray(scaled.reshape(k // 512, 128, 4, n).transpose(0, 1, 3, 2)).astype(ml_dtypes.float8_e4m3fn).view(np.uint8)
    return words, np.ascontiguousarray(byte.astype(np.uint8).reshape(k // 512, 16, n))


def unpack_weight(words, scales):
    g, p, n, _ = words.shape
    vals = np.ascontiguousarray(words).view(ml_dtypes.float8_e4m3fn).astype(np.float64) * np.repeat(np.exp2(scales.astype(np.float64) - 127.0), 8, axis=1)[..., None]
    return vals.transpose(0, 1, 3, 2).reshape(g * 512, n)

def planes(y):
    n, m = y.shape
    v = y.astype(np.float32).astype(ml_dtypes.bfloat16).astype(np.float64).reshape(n // 32, 32, m)
    top = np.abs(v).max(1)
    byte = np.clip(np.where(top > 0, np.frexp(top)[1] - 1 + 127 - 7, 1), 1, 254)
    codes = (v * np.exp2(127.0 - byte)[:, None, :]).reshape(n, m).astype(np.float32).astype(ml_dtypes.float8_e4m3fn).view(np.uint8)
    words = codes.reshape(n // 512, 128, 4, m).transpose(0, 1, 3, 2)
    return np.ascontiguousarray(words), np.ascontiguousarray(byte.astype(np.uint8).reshape(n // 512, 16, m))


K, T, S, H, C = 512, 2048, 512, 512, 512


def setup_inputs():
    n = np.random.standard_normal
    s = mx_kscale(K)[:, None]
    packed_xT = pack_weight(n((K, T)) * s)
    packed_w1 = pack_weight(n((K, H)) / np.sqrt(K) / s)
    return {
        "x_words": packed_xT[0],
        "x_scales": packed_xT[1],
        "w1_words": packed_w1[0],
        "w1_scales": packed_w1[1],
        "gs": (np.random.uniform(0.5, 1.5, (K, 1)) / s).astype(np.float32),
        "offs": striped(np.random.permutation(T)[:S]),
        "n1": striped8(np.stack([np.random.permutation(S) for _ in range(8)])),
        "n2": striped8(np.stack([np.random.permutation(S) for _ in range(8)])),
        "ca": striped(np.random.permutation(T)[:C]),
        "cb": striped(np.random.permutation(T)[:C]),
        "cd": striped(np.random.permutation(T)[:C]),
        "n3": striped8(np.stack([np.random.permutation(S) for _ in range(8)])),
        "n4": striped8(np.stack([np.random.permutation(S) for _ in range(8)])),
        "n5": striped(np.random.permutation(S)),
        "n6": striped(np.random.permutation(S)),
    }


def reference(x_words, x_scales, w1_words, w1_scales, gs, offs, n1, n2, ca, cb, cd, n3, n4, n5, n6):
    x_ca = unpack_weight(x_words, x_scales)[:, unstriped(ca)]
    xq = unpack_weight(x_words, x_scales)[:, unstriped(offs)]
    y = unpack_weight(w1_words, w1_scales).T @ xq
    st = y + 0.5 * (y[np.arange(H)[:, None], runs(n1, H)])
    z = f64(gs) * (st - (st[np.arange(H)[:, None], runs(n2, H)]))
    zq = mxq(z, 0, "e4m3")
    a = 0.0625 * (x_ca.T @ zq)
    x_cb = unpack_weight(x_words, x_scales)[:, unstriped(cb)]
    b = 0.0625 * (x_cb.T @ zq)
    m1 = np.maximum(a, b[np.arange(C)[:, None], runs(n4, C)]) - (np.minimum(a[np.arange(C)[:, None], runs(n3, C)], b))
    x_cd = unpack_weight(x_words, x_scales)[:, unstriped(cd)]
    q = 0.0625 * (x_cd.T @ zq)
    out_0 = (m1 - m1[:, unstriped(n5)]) / (np.abs(q) + np.abs(q[:, unstriped(n6)]) + 0.5)
    return (out_0,) + planes(out_0)

@@ -1,0 +1,283 @@
+from contextlib import ExitStack
+
+import concourse.mybir as mybir
+
+K, T, S, H, C = 512, 2048, 512, 512, 512
+FLOPS = 4 * 2 * 512 * 512 * 512
+
+F32 = mybir.dt.float32
+BF16 = mybir.dt.bfloat16
+I32 = mybir.dt.int32
+U32 = mybir.dt.uint32
+U16 = mybir.dt.uint16
+U8 = mybir.dt.uint8
+FP8X4 = mybir.dt.float8_e4m3fn_x4
+ALU = mybir.AluOpType
+ACT = mybir.ActivationFunctionType
+
+P = 128
+PACK = 4
+HALF = S // 2
+FUSED2 = 0
+FUSED5 = 3
+
+
+def tile_picked_tricdmaxbnormbhop_none_po_kernel(
+    tc, x_words, x_scales, w1_words, w1_scales, gs, offs, n1, n2, ca, cb, cd, n3, n4, n5, n6, out_0, out_1, out_2
+):
+    nc = tc.nc
+    with ExitStack() as ctx:
+        keep = ctx.enter_context(tc.tile_pool(name="keep", bufs=1))
+        psum = ctx.enter_context(tc.psum_pool(name="psum", bufs=8))
+
+        def sb(name, shape, dtype, tag=None):
+            return keep.tile(shape, dtype, name=name, tag=tag or name, align_bytes=64)
+
+        def load_list(name, dram):
+            tile = sb(name, [P, S // 16], U16)
+            nc.sync.dma_start(tile[:], dram)
+            return tile
+
+        def load_scales(queue, tile, dram, width):
+            rows = dram[0].bitcast(I32)
+            for quad in range(4):
+                src = rows[4 * quad : 4 * quad + 4, :].unsqueeze(0).broadcast_to([8, 4, width // 4])
+                queue.dma_start(tile[32 * quad : 32 * quad + 32, :].bitcast(I32), src)
+
+        def cols(h):
+            return slice(h * HALF, (h + 1) * HALF)
+
+        def part(lst, h):
+            return lst[:, h * (HALF // 16) : (h + 1) * (HALF // 16)]
+
+        def deal_words(name, raw):
+            dealt = sb(name, [P, S], I32)
+            nc.vector.tensor_copy(
+                dealt[:].rearrange("p (t c i) -> p c t i", t=PACK, i=4),
+                raw[:].rearrange("p (c i t) -> p c t i", t=PACK, i=4),
+            )
+            return dealt
+
+        def deal_bytes(name, raw, tag=None):
+            dealt = sb(name, [P, S], U8, tag)
+            nc.vector.tensor_copy(
+                dealt[:].rearrange("p (t c i) -> p c t i", t=PACK, i=16),
+                raw[:].rearrange("p (c i t) -> p c t i", t=PACK, i=16),
+            )
+            return dealt
+
+        xs = sb("xs", [P, T], U8)
+        load_scales(nc.sync, xs, x_scales, T)
+        l_offs = load_list("l_offs", offs)
+        l_ca = load_list("l_ca", ca)
+        xw = sb("xw", [P, T], I32)
+        nc.sync.dma_start(xw[:], x_words[0].rearrange("p n t -> p (n t)").bitcast(I32))
+        w1w = sb("w1w", [P, H], I32)
+        nc.sync.dma_start(w1w[:], w1_words[0].rearrange("p n t -> p (n t)").bitcast(I32))
+        w1s = sb("w1s", [P, H], U8)
+        load_scales(nc.sync, w1s, w1_scales, H)
+        gain = sb("gain", [P, PACK], F32)
+        nc.sync.dma_start(gain[:], gs.rearrange("(p t) o -> p (t o)", t=PACK))
+        l_n1 = load_list("l_n1", n1)
+        ngain = sb("ngain", [P, PACK], F32)
+        nc.gpsimd.tensor_scalar(ngain[:], gain[:], -1.0, 0.0, ALU.mult, ALU.add)
+        l_cd = load_list("l_cd", cd)
+        l_n2 = load_list("l_n2", n2)
+        l_cb = load_list("l_cb", cb)
+        l_n4 = load_list("l_n4", n4)
+        l_n3 = load_list("l_n3", n3)
+        l_n6 = load_list("l_n6", n6)
+        l_n5 = load_list("l_n5", n5)
+
+        def pick_words(name, lst, tag=None):
+            raw = sb(name, [P, S], I32, tag)
+            nc.vector.tensor_copy(raw[:].bitcast(U32), xw[:].bitcast(U32).indirect(lst[:]))
+            return raw
+
+        def pick_bytes(name, lst, tag=None):
+            raw = sb(name, [P, S], U8, tag)
+            nc.vector.tensor_copy(raw[:], xs[:].indirect(lst[:]))
+            return raw
+
+        def product(bank, words, scales, t, rhs_words, rhs_scales):
+            m = slice(t * P, (t + 1) * P)
+            nc.tensor.matmul_mx(
+                bank, lhsT=words[:, m].bitcast(FP8X4), lhsT_scale=scales[:, m],
+                rhs=rhs_words.bitcast(FP8X4), rhs_scale=rhs_scales, start=True, stop=True,
+            )
+
+        def gather_scalar(out, window, lst, h):
+            nc.scalar.activation(out[:, cols(h)], window[:].indirect(part(lst, h)), ACT.Copy)
+
+        xq_s = pick_bytes("xq_s", l_offs)
+        ca_s_raw = pick_bytes("ca_s_raw", l_ca)
+        xq_w = pick_words("xq_w", l_offs)
+        w1_w = deal_words("w1_w", w1w)
+        w1_s = deal_bytes("w1_s", w1s)
+        ca_s = deal_bytes("ca_s", ca_s_raw, "w1s")
+        ca_w = deal_words("ca_w", pick_words("ca_w_raw", l_ca, "w1w"))
+        cd_s = deal_bytes("cd_s", pick_bytes("cd_s_raw", l_cd))
+        cd_w = deal_words("cd_w", pick_words("cd_w_raw", l_cd))
+
+        y = [sb("y%d" % t, [P, S], F32) for t in range(PACK)]
+        g1 = [sb("g1_%d" % t, [P, S], F32) for t in range(PACK)]
+        st = [sb("st%d" % t, [P, S], F32) for t in range(PACK)]
+        g2 = [sb("g2_%d" % t, [P, S], F32) for t in range(PACK)]
+        ybank = []
+        for t in range(PACK):
+            bank = psum.tile([P, S], F32, name="bank")
+            product(bank[:], w1_w, w1_s, t, xq_w[:], xq_s[:])
+            ybank.append(bank)
+
+        def y_out(t):
+            nc.scalar.activation(y[t][:], ybank[t][:], ACT.Copy, scale=ngain[:, t : t + 1])
+
+        y_out(0)
+        for t in range(PACK):
+            if t + 1 < PACK:
+                y_out(t + 1)
+            for h in range(2):
+                gather_scalar(g1[t], y[t], l_n1, h)
+            nc.vector.scalar_tensor_tensor(st[t][:], g1[t][:], 0.5, y[t][:], ALU.mult, ALU.add)
+            if t < FUSED2:
+                nc.sync.dma_start(g2[t][:], st[t][:])
+
+        z_w, z_s = [], []
+        for h in range(2):
+            diff = sb("diff%d" % h, [P, PACK, HALF], F32)
+            for t in range(PACK):
+                if t < FUSED2:
+                    nc.vector.tensor_tensor(diff[:, t, :], st[t][:].indirect(part(l_n2, h)), g2[t][:, cols(h)], ALU.subtract)
+                else:
+                    gather_scalar(g2[t], st[t], l_n2, h)
+                    nc.vector.tensor_tensor(diff[:, t, :], g2[t][:, cols(h)], st[t][:, cols(h)], ALU.subtract)
+            zb = sb("zb%d" % h, [P, HALF * PACK], BF16)
+            nc.vector.tensor_copy(
+                zb[:].rearrange("p (c i t) -> p c t i", t=PACK, i=4),
+                diff[:].rearrange("p t (c i) -> p c t i", i=4),
+            )
+            words = sb("z_w%d" % h, [P, HALF], I32)
+            scales = sb("z_s%d" % h, [P, HALF], U8)
+            nc.vector.quantize_mx(words[:].bitcast(FP8X4), scales[:], zb[:])
+            z_w.append(words)
+            z_s.append(scales)
+
+        cb_w = deal_words("cb_w", pick_words("cb_w_raw", l_cb, "zb1"))
+        cb_s = deal_bytes("cb_s", pick_bytes("cb_s_raw", l_cb, "g1_1"))
+
+        a = [sb("a%d" % t, [P, S], F32) for t in range(PACK)]
+        b = [sb("b%d" % t, [P, S], F32) for t in range(PACK)]
+        q = [sb("q%d" % t, [P, S], F32) for t in range(PACK)]
+        q2 = [sb("q2_%d" % t, [P, S], F32) for t in range(PACK)]
+        gb = [sb("gb%d" % t, [P, S], F32) for t in range(PACK)]
+        ga = [sb("ga%d" % t, [P, S], F32) for t in range(PACK)]
+        hi = [sb("hi%d" % t, [P, S], F32) for t in range(PACK)]
+        lo = [sb("lo%d" % t, [P, S], F32) for t in range(PACK)]
+        m1 = [sb("m1_%d" % t, [P, S], F32) for t in range(PACK)]
+        m2 = [sb("m2_%d" % t, [P, S], F32) for t in range(PACK)]
+        num = [sb("num%d" % t, [P, S], F32) for t in range(PACK)]
+        den = [sb("den%d" % t, [P, S], F32) for t in range(PACK)]
+        root = [sb("root%d" % t, [P, S], F32) for t in range(PACK)]
+        inv = [sb("inv%d" % t, [P, S], F32) for t in range(PACK)]
+        res = [sb("res%d" % h, [P, PACK, HALF], F32) for h in range(2)]
+
+        qbank = [psum.tile([P, S], F32, name="bank") for t in range(PACK)]
+        abank = [psum.tile([P, S], F32, name="bank") for t in range(PACK)]
+
+        def q_half(t, h):
+            product(qbank[t][:, cols(h)], cd_w, cd_s, t, z_w[h][:], z_s[h][:])
+            nc.scalar.activation(q[t][:, cols(h)], qbank[t][:, cols(h)], ACT.Abs)
+            if h == 1:
+                nc.sync.dma_start(q2[t][:], q[t][:])
+
+        def a_half(t, h):
+            product(abank[t][:, cols(h)], ca_w, ca_s, t, z_w[h][:], z_s[h][:])
+            nc.scalar.copy(a[t][:, cols(h)], abank[t][:, cols(h)])
+
+        def a_whole(t):
+            for h in range(2):
+                product(abank[t][:, cols(h)], ca_w, ca_s, t, z_w[h][:], z_s[h][:])
+            nc.scalar.copy(a[t][:], abank[t][:])
+
+        def spread(t):
+            for h in range(2):
+                gather_scalar(ga[t], a[t], l_n3, h)
+            bank = psum.tile([P, S], F32, name="bank")
+            for h in range(2):
+                product(bank[:, cols(h)], cb_w, cb_s, t, z_w[h][:], z_s[h][:])
+            nc.scalar.copy(b[t][:], bank[:])
+            nc.vector.tensor_tensor(lo[t][:], b[t][:], ga[t][:], ALU.min)
+            for h in range(2):
+                gather_scalar(gb[t], b[t], l_n4, h)
+            nc.vector.tensor_tensor(hi[t][:], a[t][:], gb[t][:], ALU.max)
+            nc.vector.tensor_tensor(m1[t][:], lo[t][:], hi[t][:], ALU.subtract)
+            if t < FUSED5:
+                nc.sync.dma_start(m2[t][:], m1[t][:])
+
+        def q_sum(t):
+            for h in range(2):
+                nc.vector.tensor_tensor(den[t][:, cols(h)], q[t][:].indirect(part(l_n6, h)), q2[t][:, cols(h)], ALU.add)
+
+        def m_diff(t):
+            for h in range(2):
+                nc.vector.tensor_tensor(num[t][:, cols(h)], m1[t][:].indirect(part(l_n5, h)), m2[t][:, cols(h)], ALU.subtract)
+
+        def m_diff_scalar(t):
+            for h in range(2):
+                gather_scalar(m2[t], m1[t], l_n5, h)
+                nc.vector.tensor_tensor(num[t][:, cols(h)], m2[t][:, cols(h)], m1[t][:, cols(h)], ALU.subtract)
+
+        def inverse(t, c):
+            nc.scalar.activation(root[t][:, c], den[t][:, c], ACT.Abs_reciprocal_sqrt, bias=8.0)
+            nc.scalar.activation(inv[t][:, c], root[t][:, c], ACT.Square)
+
+        out_rows = out_0.rearrange("(p t) j -> p t j", t=PACK)
+
+        def finish(t, h):
+            nc.vector.tensor_tensor(res[h][:, t, :], num[t][:, cols(h)], inv[t][:, cols(h)], ALU.mult)
+            nc.sync.dma_start(out_rows[:, t, cols(h)], res[h][:, t, :])
+
+        for t in range(PACK):
+            q_half(t, 0)
+        for t in range(2):
+            a_half(t, 0)
+        for t in range(PACK):
+            q_half(t, 1)
+        for t in range(2):
+            a_half(t, 1)
+        for t in range(PACK):
+            q_sum(t)
+        spread(0)
+        spread(1)
+        a_whole(2)
+        spread(2)
+        m_diff(0)
+        a_whole(3)
+        spread(3)
+        m_diff(1)
+        inverse(0, slice(0, S))
+        inverse(1, slice(0, S))
+        m_diff(2)
+        m_diff_scalar(3)
+        for t in range(2):
+            for h in range(2):
+                finish(t, h)
+        inverse(2, slice(0, S))
+        for h in range(2):
+            finish(2, h)
+        o_s = sb("o_s", [P, S], U8)
+        out_words = out_1[0].rearrange("p n t -> p (n t)").bitcast(I32)
+        for h in range(2):
+            inverse(3, cols(h))
+            finish(3, h)
+            ob = sb("ob%d" % h, [P, HALF * PACK], BF16)
+            nc.vector.tensor_copy(
+                ob[:].rearrange("p (c i t) -> p c t i", t=PACK, i=4),
+                res[h][:].rearrange("p t (c i) -> p c t i", i=4),
+            )
+            o_w = sb("o_w%d" % h, [P, HALF], I32)
+            nc.vector.quantize_mx(o_w[:].bitcast(FP8X4), o_s[:, cols(h)], ob[:])
+            nc.sync.dma_start(out_words[:, cols(h)], o_w[:])
+        out_scales = out_2[0].bitcast(I32)
+        for quad in range(4):
+            nc.scalar.dma_start(out_scales[4 * quad : 4 * quad + 4, :], o_s[32 * quad : 32 * quad + 4, :].bitcast(I32))

@@ -18,8 +18,10 @@ ACT = mybir.ActivationFunctionType
 P = 128
 PACK = 4
 HALF = S // 2
-FUSED2 = 0
-FUSED5 = 3
+PAD = 32
+FUSED2 = 1
+FRONT = slice(0, S)
+BACK = slice(S, 2 * S)
 
 
 def tile_picked_tricdmaxbnormbhop_none_po_kernel(
@@ -38,11 +40,11 @@ def tile_picked_tricdmaxbnormbhop_none_po_kernel(
             nc.sync.dma_start(tile[:], dram)
             return tile
 
-        def load_scales(queue, tile, dram, width):
+        def load_scales(tile, dram, width):
             rows = dram[0].bitcast(I32)
             for quad in range(4):
                 src = rows[4 * quad : 4 * quad + 4, :].unsqueeze(0).broadcast_to([8, 4, width // 4])
-                queue.dma_start(tile[32 * quad : 32 * quad + 32, :].bitcast(I32), src)
+                nc.sync.dma_start(tile[32 * quad : 32 * quad + 32, :].bitcast(I32), src)
 
         def cols(h):
             return slice(h * HALF, (h + 1) * HALF)
@@ -50,8 +52,8 @@ def tile_picked_tricdmaxbnormbhop_none_po_kernel(
         def part(lst, h):
             return lst[:, h * (HALF // 16) : (h + 1) * (HALF // 16)]
 
-        def deal_words(name, raw):
-            dealt = sb(name, [P, S], I32)
+        def deal_words(name, raw, tag=None):
+            dealt = sb(name, [P, S], I32, tag)
             nc.vector.tensor_copy(
                 dealt[:].rearrange("p (t c i) -> p c t i", t=PACK, i=4),
                 raw[:].rearrange("p (c i t) -> p c t i", t=PACK, i=4),
@@ -67,7 +69,7 @@ def tile_picked_tricdmaxbnormbhop_none_po_kernel(
             return dealt
 
         xs = sb("xs", [P, T], U8)
-        load_scales(nc.sync, xs, x_scales, T)
+        load_scales(xs, x_scales, T)
         l_offs = load_list("l_offs", offs)
         l_ca = load_list("l_ca", ca)
         xw = sb("xw", [P, T], I32)
@@ -75,18 +77,16 @@ def tile_picked_tricdmaxbnormbhop_none_po_kernel(
         w1w = sb("w1w", [P, H], I32)
         nc.sync.dma_start(w1w[:], w1_words[0].rearrange("p n t -> p (n t)").bitcast(I32))
         w1s = sb("w1s", [P, H], U8)
-        load_scales(nc.sync, w1s, w1_scales, H)
+        load_scales(w1s, w1_scales, H)
         gain = sb("gain", [P, PACK], F32)
         nc.sync.dma_start(gain[:], gs.rearrange("(p t) o -> p (t o)", t=PACK))
         l_n1 = load_list("l_n1", n1)
-        ngain = sb("ngain", [P, PACK], F32)
-        nc.gpsimd.tensor_scalar(ngain[:], gain[:], -1.0, 0.0, ALU.mult, ALU.add)
         l_cd = load_list("l_cd", cd)
         l_n2 = load_list("l_n2", n2)
         l_cb = load_list("l_cb", cb)
-        l_n4 = load_list("l_n4", n4)
         l_n3 = load_list("l_n3", n3)
         l_n6 = load_list("l_n6", n6)
+        l_n4 = load_list("l_n4", n4)
         l_n5 = load_list("l_n5", n5)
 
         def pick_words(name, lst, tag=None):
@@ -106,23 +106,33 @@ def tile_picked_tricdmaxbnormbhop_none_po_kernel(
                 rhs=rhs_words.bitcast(FP8X4), rhs_scale=rhs_scales, start=True, stop=True,
             )
 
-        def gather_scalar(out, window, lst, h):
-            nc.scalar.activation(out[:, cols(h)], window[:].indirect(part(lst, h)), ACT.Copy)
+        def fetch(out, window, offsets):
+            nc.scalar.activation(out, window[:].indirect(offsets), ACT.Copy)
+
+        ya = [sb("ya%d" % t, [P, 2 * S], F32) for t in range(PACK)]
+        q = [sb("q%d" % t, [P, S + PAD], F32) for t in range(PACK)]
+        warm = sb("warm", [P, 1], F32)
+        nc.gpsimd.memset(warm[:], 1.0)
+        warm_out = sb("warm_out", [P, 1], F32)
+        nc.scalar.activation(warm_out[:], warm[:], ACT.Abs_reciprocal_sqrt, bias=8.0)
+        for t in range(PACK):
+            nc.gpsimd.memset(ya[t][:, BACK], 0.0)
+        for t in range(PACK):
+            nc.gpsimd.memset(q[t][:, S:], 0.0)
 
         xq_s = pick_bytes("xq_s", l_offs)
         ca_s_raw = pick_bytes("ca_s_raw", l_ca)
         xq_w = pick_words("xq_w", l_offs)
         w1_w = deal_words("w1_w", w1w)
         w1_s = deal_bytes("w1_s", w1s)
-        ca_s = deal_bytes("ca_s", ca_s_raw, "w1s")
-        ca_w = deal_words("ca_w", pick_words("ca_w_raw", l_ca, "w1w"))
+        ca_s = deal_bytes("ca_s", ca_s_raw, "w1w")
+        ca_w = deal_words("ca_w", pick_words("ca_w_raw", l_ca, "w1s"))
         cd_s = deal_bytes("cd_s", pick_bytes("cd_s_raw", l_cd))
         cd_w = deal_words("cd_w", pick_words("cd_w_raw", l_cd))
 
-        y = [sb("y%d" % t, [P, S], F32) for t in range(PACK)]
         g1 = [sb("g1_%d" % t, [P, S], F32) for t in range(PACK)]
         st = [sb("st%d" % t, [P, S], F32) for t in range(PACK)]
-        g2 = [sb("g2_%d" % t, [P, S], F32) for t in range(PACK)]
+        st2 = [sb("st2_%d" % t, [P, S], F32) for t in range(FUSED2)]
         ybank = []
         for t in range(PACK):
             bank = psum.tile([P, S], F32, name="bank")
@@ -130,27 +140,27 @@ def tile_picked_tricdmaxbnormbhop_none_po_kernel(
             ybank.append(bank)
 
         def y_out(t):
-            nc.scalar.activation(y[t][:], ybank[t][:], ACT.Copy, scale=ngain[:, t : t + 1])
+            nc.scalar.activation(ya[t][:, FRONT], ybank[t][:], ACT.Copy, scale=gain[:, t : t + 1])
 
         y_out(0)
         for t in range(PACK):
             if t + 1 < PACK:
                 y_out(t + 1)
-            for h in range(2):
-                gather_scalar(g1[t], y[t], l_n1, h)
-            nc.vector.scalar_tensor_tensor(st[t][:], g1[t][:], 0.5, y[t][:], ALU.mult, ALU.add)
+            fetch(g1[t][:], ya[t], l_n1[:])
+            nc.vector.scalar_tensor_tensor(st[t][:], g1[t][:], 0.5, ya[t][:, FRONT], ALU.mult, ALU.add)
             if t < FUSED2:
-                nc.sync.dma_start(g2[t][:], st[t][:])
+                nc.sync.dma_start(st2[t][:], st[t][:])
 
         z_w, z_s = [], []
         for h in range(2):
-            diff = sb("diff%d" % h, [P, PACK, HALF], F32)
+            g2 = sb("g2_%d" % h, [P, PACK - FUSED2, HALF], F32, "g1_3" if h else None)
+            diff = sb("diff%d" % h, [P, PACK, HALF], F32, "diff")
             for t in range(PACK):
                 if t < FUSED2:
-                    nc.vector.tensor_tensor(diff[:, t, :], st[t][:].indirect(part(l_n2, h)), g2[t][:, cols(h)], ALU.subtract)
+                    nc.vector.tensor_tensor(diff[:, t, :], st[t][:].indirect(part(l_n2, h)), st2[t][:, cols(h)], ALU.subtract)
                 else:
-                    gather_scalar(g2[t], st[t], l_n2, h)
-                    nc.vector.tensor_tensor(diff[:, t, :], g2[t][:, cols(h)], st[t][:, cols(h)], ALU.subtract)
+                    fetch(g2[:, t - FUSED2, :], st[t], part(l_n2, h))
+                    nc.vector.tensor_tensor(diff[:, t, :], g2[:, t - FUSED2, :], st[t][:, cols(h)], ALU.subtract)
             zb = sb("zb%d" % h, [P, HALF * PACK], BF16)
             nc.vector.tensor_copy(
                 zb[:].rearrange("p (c i t) -> p c t i", t=PACK, i=4),
@@ -162,25 +172,22 @@ def tile_picked_tricdmaxbnormbhop_none_po_kernel(
             z_w.append(words)
             z_s.append(scales)
 
-        cb_w = deal_words("cb_w", pick_words("cb_w_raw", l_cb, "zb1"))
-        cb_s = deal_bytes("cb_s", pick_bytes("cb_s_raw", l_cb, "g1_1"))
+        cb_w_raw = pick_words("cb_w_raw", l_cb, "zb1")
+        cb_s_raw = pick_bytes("cb_s_raw", l_cb, "diff")
+        cb_w = deal_words("cb_w", cb_w_raw)
+        cb_s = deal_bytes("cb_s", cb_s_raw)
 
-        a = [sb("a%d" % t, [P, S], F32) for t in range(PACK)]
-        b = [sb("b%d" % t, [P, S], F32) for t in range(PACK)]
-        q = [sb("q%d" % t, [P, S], F32) for t in range(PACK)]
+        bga = [sb("bga%d" % t, [P, 2 * S], F32) for t in range(PACK)]
         q2 = [sb("q2_%d" % t, [P, S], F32) for t in range(PACK)]
         gb = [sb("gb%d" % t, [P, S], F32) for t in range(PACK)]
-        ga = [sb("ga%d" % t, [P, S], F32) for t in range(PACK)]
         hi = [sb("hi%d" % t, [P, S], F32) for t in range(PACK)]
-        lo = [sb("lo%d" % t, [P, S], F32) for t in range(PACK)]
-        m1 = [sb("m1_%d" % t, [P, S], F32) for t in range(PACK)]
+        mlo = [sb("mlo%d" % t, [P, 2 * S], F32, "q2_%d" % t) for t in range(PACK)]
         m2 = [sb("m2_%d" % t, [P, S], F32) for t in range(PACK)]
         num = [sb("num%d" % t, [P, S], F32) for t in range(PACK)]
         den = [sb("den%d" % t, [P, S], F32) for t in range(PACK)]
         root = [sb("root%d" % t, [P, S], F32) for t in range(PACK)]
         inv = [sb("inv%d" % t, [P, S], F32) for t in range(PACK)]
         res = [sb("res%d" % h, [P, PACK, HALF], F32) for h in range(2)]
-
         qbank = [psum.tile([P, S], F32, name="bank") for t in range(PACK)]
         abank = [psum.tile([P, S], F32, name="bank") for t in range(PACK)]
 
@@ -188,44 +195,39 @@ def tile_picked_tricdmaxbnormbhop_none_po_kernel(
             product(qbank[t][:, cols(h)], cd_w, cd_s, t, z_w[h][:], z_s[h][:])
             nc.scalar.activation(q[t][:, cols(h)], qbank[t][:, cols(h)], ACT.Abs)
             if h == 1:
-                nc.sync.dma_start(q2[t][:], q[t][:])
+                nc.sync.dma_start(q2[t][:], q[t][:, FRONT])
 
-        def a_half(t, h):
+        def a_half(t, h, copy):
             product(abank[t][:, cols(h)], ca_w, ca_s, t, z_w[h][:], z_s[h][:])
-            nc.scalar.copy(a[t][:, cols(h)], abank[t][:, cols(h)])
+            copy(ya[t][:, cols(h)], abank[t][:, cols(h)])
 
-        def a_whole(t):
+        def a_whole(t, copy):
             for h in range(2):
                 product(abank[t][:, cols(h)], ca_w, ca_s, t, z_w[h][:], z_s[h][:])
-            nc.scalar.copy(a[t][:], abank[t][:])
+            copy(ya[t][:, FRONT], abank[t][:])
 
-        def spread(t):
-            for h in range(2):
-                gather_scalar(ga[t], a[t], l_n3, h)
+        def spread(t, fused, bcopy):
+            fetch(bga[t][:, BACK], ya[t], l_n3[:])
             bank = psum.tile([P, S], F32, name="bank")
             for h in range(2):
                 product(bank[:, cols(h)], cb_w, cb_s, t, z_w[h][:], z_s[h][:])
-            nc.scalar.copy(b[t][:], bank[:])
-            nc.vector.tensor_tensor(lo[t][:], b[t][:], ga[t][:], ALU.min)
-            for h in range(2):
-                gather_scalar(gb[t], b[t], l_n4, h)
-            nc.vector.tensor_tensor(hi[t][:], a[t][:], gb[t][:], ALU.max)
-            nc.vector.tensor_tensor(m1[t][:], lo[t][:], hi[t][:], ALU.subtract)
-            if t < FUSED5:
-                nc.sync.dma_start(m2[t][:], m1[t][:])
+            bcopy(bga[t][:, FRONT], bank[:])
+            nc.vector.tensor_tensor(mlo[t][:, BACK], bga[t][:, FRONT], bga[t][:, BACK], ALU.max)
+            fetch(gb[t][:], bga[t], l_n4[:])
+            nc.vector.tensor_tensor(hi[t][:], ya[t][:, FRONT], gb[t][:], ALU.min)
+            nc.vector.tensor_tensor(mlo[t][:, FRONT], hi[t][:], mlo[t][:, BACK], ALU.subtract)
+            if fused:
+                nc.sync.dma_start(m2[t][:], mlo[t][:, FRONT])
 
         def q_sum(t):
-            for h in range(2):
-                nc.vector.tensor_tensor(den[t][:, cols(h)], q[t][:].indirect(part(l_n6, h)), q2[t][:, cols(h)], ALU.add)
+            nc.vector.tensor_tensor(den[t][:], q[t][:].indirect(l_n6[:]), q2[t][:], ALU.add)
 
         def m_diff(t):
-            for h in range(2):
-                nc.vector.tensor_tensor(num[t][:, cols(h)], m1[t][:].indirect(part(l_n5, h)), m2[t][:, cols(h)], ALU.subtract)
+            nc.vector.tensor_tensor(num[t][:], mlo[t][:].indirect(l_n5[:]), m2[t][:], ALU.subtract)
 
-        def m_diff_scalar(t):
-            for h in range(2):
-                gather_scalar(m2[t], m1[t], l_n5, h)
-                nc.vector.tensor_tensor(num[t][:, cols(h)], m2[t][:, cols(h)], m1[t][:, cols(h)], ALU.subtract)
+        def m_diff_scalar(t, h):
+            fetch(m2[t][:, cols(h)], mlo[t], part(l_n5, h))
+            nc.vector.tensor_tensor(num[t][:, cols(h)], m2[t][:, cols(h)], mlo[t][:, cols(h)], ALU.subtract)
 
         def inverse(t, c):
             nc.scalar.activation(root[t][:, c], den[t][:, c], ACT.Abs_reciprocal_sqrt, bias=8.0)
@@ -237,47 +239,52 @@ def tile_picked_tricdmaxbnormbhop_none_po_kernel(
             nc.vector.tensor_tensor(res[h][:, t, :], num[t][:, cols(h)], inv[t][:, cols(h)], ALU.mult)
             nc.sync.dma_start(out_rows[:, t, cols(h)], res[h][:, t, :])
 
-        for t in range(PACK):
-            q_half(t, 0)
-        for t in range(2):
-            a_half(t, 0)
-        for t in range(PACK):
-            q_half(t, 1)
-        for t in range(2):
-            a_half(t, 1)
-        for t in range(PACK):
-            q_sum(t)
-        spread(0)
-        spread(1)
-        a_whole(2)
-        spread(2)
-        m_diff(0)
-        a_whole(3)
-        spread(3)
-        m_diff(1)
-        inverse(0, slice(0, S))
-        inverse(1, slice(0, S))
-        m_diff(2)
-        m_diff_scalar(3)
-        for t in range(2):
-            for h in range(2):
-                finish(t, h)
-        inverse(2, slice(0, S))
-        for h in range(2):
-            finish(2, h)
         o_s = sb("o_s", [P, S], U8)
         out_words = out_1[0].rearrange("p n t -> p (n t)").bitcast(I32)
-        for h in range(2):
-            inverse(3, cols(h))
-            finish(3, h)
+
+        def planes(h, copy):
             ob = sb("ob%d" % h, [P, HALF * PACK], BF16)
-            nc.vector.tensor_copy(
+            copy(
                 ob[:].rearrange("p (c i t) -> p c t i", t=PACK, i=4),
                 res[h][:].rearrange("p t (c i) -> p c t i", i=4),
             )
             o_w = sb("o_w%d" % h, [P, HALF], I32)
             nc.vector.quantize_mx(o_w[:].bitcast(FP8X4), o_s[:, cols(h)], ob[:])
             nc.sync.dma_start(out_words[:, cols(h)], o_w[:])
+
+        on_v, on_s = nc.vector.tensor_copy, nc.scalar.copy
+        for t in range(PACK):
+            q_half(t, 0)
+        for t in range(PACK):
+            a_half(t, 0, on_s)
+        for t in range(PACK):
+            q_half(t, 1)
+        for t in range(PACK):
+            a_half(t, 1, on_s)
+        q_sum(0)
+        q_sum(1)
+        spread(0, True, on_s)
+        q_sum(2)
+        spread(1, True, on_s)
+        q_sum(3)
+        spread(2, False, on_s)
+        inverse(0, FRONT)
+        m_diff(0)
+        spread(3, False, on_s)
+        m_diff(1)
+        inverse(1, FRONT)
+        for h in range(2):
+            m_diff_scalar(2, h)
+        inverse(2, FRONT)
+        inverse(3, FRONT)
+        for t in range(PACK - 1):
+            for h in range(2):
+                finish(t, h)
+        for h in range(2):
+            m_diff_scalar(3, h)
+            finish(3, h)
+        planes(0, on_s)
+        planes(1, on_v)
         out_scales = out_2[0].bitcast(I32)
         for quad in range(4):
             nc.scalar.dma_start(out_scales[4 * quad : 4 * quad + 4, :], o_s[32 * quad : 32 * quad + 4, :].bitcast(I32))

@@ -128,7 +128,6 @@ def tile_picked_tricdmaxbnormbhop_none_po_kernel(
         ca_s = deal_bytes("ca_s", ca_s_raw, "w1w")
         ca_w = deal_words("ca_w", pick_words("ca_w_raw", l_ca, "w1s"))
         cd_s = deal_bytes("cd_s", pick_bytes("cd_s_raw", l_cd))
-        cd_w = deal_words("cd_w", pick_words("cd_w_raw", l_cd))
 
         g1 = [sb("g1_%d" % t, [P, S], F32) for t in range(PACK)]
         st = [sb("st%d" % t, [P, S], F32) for t in range(PACK)]
@@ -149,7 +148,9 @@ def tile_picked_tricdmaxbnormbhop_none_po_kernel(
             fetch(g1[t][:], ya[t], l_n1[:])
             nc.vector.scalar_tensor_tensor(st[t][:], g1[t][:], 0.5, ya[t][:, FRONT], ALU.mult, ALU.add)
             if t < FUSED2:
-                nc.sync.dma_start(st2[t][:], st[t][:])
+                nc.vector.tensor_copy(st2[t][:], st[t][:])
+            if t == 0:
+                cd_w = deal_words("cd_w", pick_words("cd_w_raw", l_cd, "g1_0"))
 
         z_w, z_s = [], []
         for h in range(2):
@@ -187,7 +188,7 @@ def tile_picked_tricdmaxbnormbhop_none_po_kernel(
         den = [sb("den%d" % t, [P, S], F32) for t in range(PACK)]
         root = [sb("root%d" % t, [P, S], F32) for t in range(PACK)]
         inv = [sb("inv%d" % t, [P, S], F32) for t in range(PACK)]
-        res = [sb("res%d" % h, [P, PACK, HALF], F32) for h in range(2)]
+        res = sb("res", [P, PACK, S], F32)
         qbank = [psum.tile([P, S], F32, name="bank") for t in range(PACK)]
         abank = [psum.tile([P, S], F32, name="bank") for t in range(PACK)]
 
@@ -229,15 +230,19 @@ def tile_picked_tricdmaxbnormbhop_none_po_kernel(
             fetch(m2[t][:, cols(h)], mlo[t], part(l_n5, h))
             nc.vector.tensor_tensor(num[t][:, cols(h)], m2[t][:, cols(h)], mlo[t][:, cols(h)], ALU.subtract)
 
+        def m_diff_whole(t):
+            fetch(m2[t][:], mlo[t], l_n5[:])
+            nc.vector.tensor_tensor(num[t][:], m2[t][:], mlo[t][:, FRONT], ALU.subtract)
+
         def inverse(t, c):
             nc.scalar.activation(root[t][:, c], den[t][:, c], ACT.Abs_reciprocal_sqrt, bias=8.0)
             nc.scalar.activation(inv[t][:, c], root[t][:, c], ACT.Square)
 
         out_rows = out_0.rearrange("(p t) j -> p t j", t=PACK)
 
-        def finish(t, h):
-            nc.vector.tensor_tensor(res[h][:, t, :], num[t][:, cols(h)], inv[t][:, cols(h)], ALU.mult)
-            nc.sync.dma_start(out_rows[:, t, cols(h)], res[h][:, t, :])
+        def finish(t, c):
+            nc.vector.tensor_tensor(res[:, t, c], num[t][:, c], inv[t][:, c], ALU.mult)
+            nc.sync.dma_start(out_rows[:, t, c], res[:, t, c])
 
         o_s = sb("o_s", [P, S], U8)
         out_words = out_1[0].rearrange("p n t -> p (n t)").bitcast(I32)
@@ -246,43 +251,40 @@ def tile_picked_tricdmaxbnormbhop_none_po_kernel(
             ob = sb("ob%d" % h, [P, HALF * PACK], BF16)
             copy(
                 ob[:].rearrange("p (c i t) -> p c t i", t=PACK, i=4),
-                res[h][:].rearrange("p t (c i) -> p c t i", i=4),
+                res[:, :, cols(h)].rearrange("p t (c i) -> p c t i", i=4),
             )
             o_w = sb("o_w%d" % h, [P, HALF], I32)
             nc.vector.quantize_mx(o_w[:].bitcast(FP8X4), o_s[:, cols(h)], ob[:])
             nc.sync.dma_start(out_words[:, cols(h)], o_w[:])
 
         on_v, on_s = nc.vector.tensor_copy, nc.scalar.copy
-        for t in range(PACK):
-            q_half(t, 0)
-        for t in range(PACK):
-            a_half(t, 0, on_s)
-        for t in range(PACK):
-            q_half(t, 1)
-        for t in range(PACK):
-            a_half(t, 1, on_s)
+        for h in range(2):
+            for t in range(PACK):
+                q_half(t, h)
+        for h in range(2):
+            for t in range(PACK):
+                a_half(t, h, on_s if t + h <= 3 else on_v)
         q_sum(0)
         q_sum(1)
         spread(0, True, on_s)
         q_sum(2)
         spread(1, True, on_s)
         q_sum(3)
-        spread(2, False, on_s)
-        inverse(0, FRONT)
+        spread(2, True, on_s)
         m_diff(0)
         spread(3, False, on_s)
         m_diff(1)
+        inverse(0, FRONT)
+        finish(0, FRONT)
         inverse(1, FRONT)
-        for h in range(2):
-            m_diff_scalar(2, h)
+        finish(1, FRONT)
+        m_diff(2)
         inverse(2, FRONT)
+        finish(2, FRONT)
         inverse(3, FRONT)
-        for t in range(PACK - 1):
-            for h in range(2):
-                finish(t, h)
         for h in range(2):
             m_diff_scalar(3, h)
-            finish(3, h)
+            finish(3, cols(h))
         planes(0, on_s)
         planes(1, on_v)
         out_scales = out_2[0].bitcast(I32)

@@ -2,7 +2,7 @@ from contextlib import ExitStack
 
 import concourse.mybir as mybir
 
-K, T, S, H, C = 512, 2048, 512, 512, 512
+T, S, H = 2048, 512, 512
 FLOPS = 4 * 2 * 512 * 512 * 512
 
 F32 = mybir.dt.float32
@@ -17,11 +17,15 @@ ACT = mybir.ActivationFunctionType
 
 P = 128
 PACK = 4
+LAST = PACK - 1
+QUADS = 4
+PER_COLUMN = 16
+LINE_WORDS, LINE_BYTES = 4, 16
 HALF = S // 2
 PAD = 32
-FUSED2 = 1
 FRONT = slice(0, S)
 BACK = slice(S, 2 * S)
+BIAS = 8.0
 
 
 def tile_picked_tricdmaxbnormbhop_none_po_kernel(
@@ -32,41 +36,42 @@ def tile_picked_tricdmaxbnormbhop_none_po_kernel(
         keep = ctx.enter_context(tc.tile_pool(name="keep", bufs=1))
         psum = ctx.enter_context(tc.psum_pool(name="psum", bufs=8))
 
-        def sb(name, shape, dtype, tag=None):
-            return keep.tile(shape, dtype, name=name, tag=tag or name, align_bytes=64)
+        def sb(name, shape, dtype, reuse=None):
+            return keep.tile(shape, dtype, name=name, tag=reuse or name, align_bytes=64)
+
+        def row_tiles(name, width, reuse=None):
+            return [sb("%s%d" % (name, t), [P, width], F32, reuse and "%s%d" % (reuse, t)) for t in range(PACK)]
 
         def load_list(name, dram):
-            tile = sb(name, [P, S // 16], U16)
+            tile = sb(name, [P, S // PER_COLUMN], U16)
             nc.sync.dma_start(tile[:], dram)
             return tile
 
         def load_scales(tile, dram, width):
             rows = dram[0].bitcast(I32)
-            for quad in range(4):
+            for quad in range(QUADS):
                 src = rows[4 * quad : 4 * quad + 4, :].unsqueeze(0).broadcast_to([8, 4, width // 4])
                 nc.sync.dma_start(tile[32 * quad : 32 * quad + 32, :].bitcast(I32), src)
 
         def cols(h):
             return slice(h * HALF, (h + 1) * HALF)
 
-        def part(lst, h):
-            return lst[:, h * (HALF // 16) : (h + 1) * (HALF // 16)]
+        def entries(lst, h):
+            return lst[:, h * (HALF // PER_COLUMN) : (h + 1) * (HALF // PER_COLUMN)]
 
-        def deal_words(name, raw, tag=None):
-            dealt = sb(name, [P, S], I32, tag)
+        def deal(name, raw, dtype, run, reuse=None):
+            dealt = sb(name, [P, S], dtype, reuse)
             nc.vector.tensor_copy(
-                dealt[:].rearrange("p (t c i) -> p c t i", t=PACK, i=4),
-                raw[:].rearrange("p (c i t) -> p c t i", t=PACK, i=4),
+                dealt[:].rearrange("p (t c i) -> p c t i", t=PACK, i=run),
+                raw[:].rearrange("p (c i t) -> p c t i", t=PACK, i=run),
             )
             return dealt
 
-        def deal_bytes(name, raw, tag=None):
-            dealt = sb(name, [P, S], U8, tag)
-            nc.vector.tensor_copy(
-                dealt[:].rearrange("p (t c i) -> p c t i", t=PACK, i=16),
-                raw[:].rearrange("p (c i t) -> p c t i", t=PACK, i=16),
-            )
-            return dealt
+        def deal_words(name, raw):
+            return deal(name, raw, I32, LINE_WORDS)
+
+        def deal_bytes(name, raw, reuse=None):
+            return deal(name, raw, U8, LINE_BYTES, reuse)
 
         xs = sb("xs", [P, T], U8)
         load_scales(xs, x_scales, T)
@@ -89,13 +94,13 @@ def tile_picked_tricdmaxbnormbhop_none_po_kernel(
         l_n4 = load_list("l_n4", n4)
         l_n5 = load_list("l_n5", n5)
 
-        def pick_words(name, lst, tag=None):
-            raw = sb(name, [P, S], I32, tag)
+        def pick_words(name, lst, reuse=None):
+            raw = sb(name, [P, S], I32, reuse)
             nc.vector.tensor_copy(raw[:].bitcast(U32), xw[:].bitcast(U32).indirect(lst[:]))
             return raw
 
-        def pick_bytes(name, lst, tag=None):
-            raw = sb(name, [P, S], U8, tag)
+        def pick_bytes(name, lst, reuse=None):
+            raw = sb(name, [P, S], U8, reuse)
             nc.vector.tensor_copy(raw[:], xs[:].indirect(lst[:]))
             return raw
 
@@ -109,12 +114,20 @@ def tile_picked_tricdmaxbnormbhop_none_po_kernel(
         def fetch(out, window, offsets):
             nc.scalar.activation(out, window[:].indirect(offsets), ACT.Copy)
 
-        ya = [sb("ya%d" % t, [P, 2 * S], F32) for t in range(PACK)]
-        q = [sb("q%d" % t, [P, S + PAD], F32) for t in range(PACK)]
+        def interleave(copy, name, values):
+            rounded = sb(name, [P, HALF * PACK], BF16)
+            copy(
+                rounded[:].rearrange("p (c i t) -> p c t i", t=PACK, i=LINE_WORDS),
+                values.rearrange("p t (c i) -> p c t i", i=LINE_WORDS),
+            )
+            return rounded
+
+        ya = row_tiles("ya", 2 * S)
+        q = row_tiles("q", S + PAD)
         warm = sb("warm", [P, 1], F32)
         nc.gpsimd.memset(warm[:], 1.0)
         warm_out = sb("warm_out", [P, 1], F32)
-        nc.scalar.activation(warm_out[:], warm[:], ACT.Abs_reciprocal_sqrt, bias=8.0)
+        nc.scalar.activation(warm_out[:], warm[:], ACT.Abs_reciprocal_sqrt, bias=BIAS)
         for t in range(PACK):
             nc.gpsimd.memset(ya[t][:, BACK], 0.0)
         for t in range(PACK):
@@ -129,9 +142,9 @@ def tile_picked_tricdmaxbnormbhop_none_po_kernel(
         ca_w = deal_words("ca_w", pick_words("ca_w_raw", l_ca, "w1s"))
         cd_s = deal_bytes("cd_s", pick_bytes("cd_s_raw", l_cd))
 
-        g1 = [sb("g1_%d" % t, [P, S], F32) for t in range(PACK)]
-        st = [sb("st%d" % t, [P, S], F32) for t in range(PACK)]
-        st2 = [sb("st2_%d" % t, [P, S], F32) for t in range(FUSED2)]
+        y_n1 = row_tiles("y_n1_", S)
+        st = row_tiles("st", S)
+        st0_twin = sb("st0_twin", [P, S], F32)
         ybank = []
         for t in range(PACK):
             bank = psum.tile([P, S], F32, name="bank")
@@ -143,100 +156,75 @@ def tile_picked_tricdmaxbnormbhop_none_po_kernel(
 
         y_out(0)
         for t in range(PACK):
-            if t + 1 < PACK:
+            if t < LAST:
                 y_out(t + 1)
-            fetch(g1[t][:], ya[t], l_n1[:])
-            nc.vector.scalar_tensor_tensor(st[t][:], g1[t][:], 0.5, ya[t][:, FRONT], ALU.mult, ALU.add)
-            if t < FUSED2:
-                nc.vector.tensor_copy(st2[t][:], st[t][:])
+            fetch(y_n1[t][:], ya[t], l_n1[:])
+            nc.vector.scalar_tensor_tensor(st[t][:], y_n1[t][:], 0.5, ya[t][:, FRONT], ALU.mult, ALU.add)
             if t == 0:
-                cd_w = deal_words("cd_w", pick_words("cd_w_raw", l_cd, "g1_0"))
+                nc.vector.tensor_copy(st0_twin[:], st[0][:])
+                cd_w = deal_words("cd_w", pick_words("cd_w_raw", l_cd, "y_n1_0"))
 
         z_w, z_s = [], []
         for h in range(2):
-            g2 = sb("g2_%d" % h, [P, PACK - FUSED2, HALF], F32, "g1_3" if h else None)
+            st_n2 = sb("st_n2_%d" % h, [P, LAST, HALF], F32, "y_n1_%d" % LAST if h else None)
             diff = sb("diff%d" % h, [P, PACK, HALF], F32, "diff")
-            for t in range(PACK):
-                if t < FUSED2:
-                    nc.vector.tensor_tensor(diff[:, t, :], st[t][:].indirect(part(l_n2, h)), st2[t][:, cols(h)], ALU.subtract)
-                else:
-                    fetch(g2[:, t - FUSED2, :], st[t], part(l_n2, h))
-                    nc.vector.tensor_tensor(diff[:, t, :], g2[:, t - FUSED2, :], st[t][:, cols(h)], ALU.subtract)
-            zb = sb("zb%d" % h, [P, HALF * PACK], BF16)
-            nc.vector.tensor_copy(
-                zb[:].rearrange("p (c i t) -> p c t i", t=PACK, i=4),
-                diff[:].rearrange("p t (c i) -> p c t i", i=4),
+            nc.vector.tensor_tensor(
+                diff[:, 0, :], st[0][:].indirect(entries(l_n2, h)), st0_twin[:, cols(h)], ALU.subtract
             )
+            for t in range(1, PACK):
+                fetch(st_n2[:, t - 1, :], st[t], entries(l_n2, h))
+                nc.vector.tensor_tensor(diff[:, t, :], st_n2[:, t - 1, :], st[t][:, cols(h)], ALU.subtract)
+            z_bf = interleave(nc.vector.tensor_copy, "z_bf%d" % h, diff[:])
             words = sb("z_w%d" % h, [P, HALF], I32)
             scales = sb("z_s%d" % h, [P, HALF], U8)
-            nc.vector.quantize_mx(words[:].bitcast(FP8X4), scales[:], zb[:])
+            nc.vector.quantize_mx(words[:].bitcast(FP8X4), scales[:], z_bf[:])
             z_w.append(words)
             z_s.append(scales)
 
-        cb_w_raw = pick_words("cb_w_raw", l_cb, "zb1")
+        cb_w_raw = pick_words("cb_w_raw", l_cb, "z_bf1")
         cb_s_raw = pick_bytes("cb_s_raw", l_cb, "diff")
         cb_w = deal_words("cb_w", cb_w_raw)
         cb_s = deal_bytes("cb_s", cb_s_raw)
 
-        bga = [sb("bga%d" % t, [P, 2 * S], F32) for t in range(PACK)]
-        q2 = [sb("q2_%d" % t, [P, S], F32) for t in range(PACK)]
-        gb = [sb("gb%d" % t, [P, S], F32) for t in range(PACK)]
-        hi = [sb("hi%d" % t, [P, S], F32) for t in range(PACK)]
-        mlo = [sb("mlo%d" % t, [P, 2 * S], F32, "q2_%d" % t) for t in range(PACK)]
-        m2 = [sb("m2_%d" % t, [P, S], F32) for t in range(PACK)]
-        num = [sb("num%d" % t, [P, S], F32) for t in range(PACK)]
-        den = [sb("den%d" % t, [P, S], F32) for t in range(PACK)]
-        root = [sb("root%d" % t, [P, S], F32) for t in range(PACK)]
-        inv = [sb("inv%d" % t, [P, S], F32) for t in range(PACK)]
+        b_an3 = row_tiles("b_an3_", 2 * S)
+        q_twin = row_tiles("q_twin", S)
+        b_n4 = row_tiles("b_n4_", S)
+        upper = row_tiles("upper", S)
+        m_lower = row_tiles("m_lower", 2 * S, "q_twin")
+        m_other = row_tiles("m_other", S)
+        num = row_tiles("num", S)
+        den = row_tiles("den", S)
+        root = row_tiles("root", S)
+        inv = row_tiles("inv", S)
         res = sb("res", [P, PACK, S], F32)
         qbank = [psum.tile([P, S], F32, name="bank") for t in range(PACK)]
         abank = [psum.tile([P, S], F32, name="bank") for t in range(PACK)]
 
-        def q_half(t, h):
-            product(qbank[t][:, cols(h)], cd_w, cd_s, t, z_w[h][:], z_s[h][:])
-            nc.scalar.activation(q[t][:, cols(h)], qbank[t][:, cols(h)], ACT.Abs)
-            if h == 1:
-                nc.sync.dma_start(q2[t][:], q[t][:, FRONT])
-
-        def a_half(t, h, copy):
-            product(abank[t][:, cols(h)], ca_w, ca_s, t, z_w[h][:], z_s[h][:])
-            copy(ya[t][:, cols(h)], abank[t][:, cols(h)])
-
-        def a_whole(t, copy):
-            for h in range(2):
-                product(abank[t][:, cols(h)], ca_w, ca_s, t, z_w[h][:], z_s[h][:])
-            copy(ya[t][:, FRONT], abank[t][:])
-
-        def spread(t, fused, bcopy):
-            fetch(bga[t][:, BACK], ya[t], l_n3[:])
-            bank = psum.tile([P, S], F32, name="bank")
-            for h in range(2):
-                product(bank[:, cols(h)], cb_w, cb_s, t, z_w[h][:], z_s[h][:])
-            bcopy(bga[t][:, FRONT], bank[:])
-            nc.vector.tensor_tensor(mlo[t][:, BACK], bga[t][:, FRONT], bga[t][:, BACK], ALU.max)
-            fetch(gb[t][:], bga[t], l_n4[:])
-            nc.vector.tensor_tensor(hi[t][:], ya[t][:, FRONT], gb[t][:], ALU.min)
-            nc.vector.tensor_tensor(mlo[t][:, FRONT], hi[t][:], mlo[t][:, BACK], ALU.subtract)
-            if fused:
-                nc.sync.dma_start(m2[t][:], mlo[t][:, FRONT])
+        bbank = [psum.tile([P, S], F32, name="bank") for t in range(PACK)]
 
         def q_sum(t):
-            nc.vector.tensor_tensor(den[t][:], q[t][:].indirect(l_n6[:]), q2[t][:], ALU.add)
+            nc.vector.tensor_tensor(den[t][:], q[t][:].indirect(l_n6[:]), q_twin[t][:], ALU.add)
+
+        def b_out(t):
+            for h in range(2):
+                product(bbank[t][:, cols(h)], cb_w, cb_s, t, z_w[h][:], z_s[h][:])
+            (nc.vector.tensor_copy if t in (0,1) else nc.scalar.copy)(b_an3[t][:, FRONT], bbank[t][:])
+
+        def spread(t):
+            fetch(b_an3[t][:, BACK], ya[t], l_n3[:])
+            nc.vector.tensor_tensor(m_lower[t][:, BACK], bbank[t][:], b_an3[t][:, BACK], ALU.max)
+            fetch(b_n4[t][:], b_an3[t], l_n4[:])
+            nc.vector.tensor_tensor(upper[t][:], abank[t][:], b_n4[t][:], ALU.min)
+            (nc.gpsimd if t in (0,1,2) else nc.vector).tensor_tensor(m_lower[t][:, FRONT], upper[t][:], m_lower[t][:, BACK], ALU.subtract)
+            if t < 2:
+                nc.sync.dma_start(m_other[t][:], m_lower[t][:, FRONT])
 
         def m_diff(t):
-            nc.vector.tensor_tensor(num[t][:], mlo[t][:].indirect(l_n5[:]), m2[t][:], ALU.subtract)
+            nc.vector.tensor_tensor(num[t][:], m_lower[t][:].indirect(l_n5[:]), m_other[t][:], ALU.subtract)
 
-        def m_diff_scalar(t, h):
-            fetch(m2[t][:, cols(h)], mlo[t], part(l_n5, h))
-            nc.vector.tensor_tensor(num[t][:, cols(h)], m2[t][:, cols(h)], mlo[t][:, cols(h)], ALU.subtract)
-
-        def m_diff_whole(t):
-            fetch(m2[t][:], mlo[t], l_n5[:])
-            nc.vector.tensor_tensor(num[t][:], m2[t][:], mlo[t][:, FRONT], ALU.subtract)
-
-        def inverse(t, c):
-            nc.scalar.activation(root[t][:, c], den[t][:, c], ACT.Abs_reciprocal_sqrt, bias=8.0)
-            nc.scalar.activation(inv[t][:, c], root[t][:, c], ACT.Square)
+        def inverse(t):
+            nc.scalar.activation(root[t][:], den[t][:], ACT.Abs_reciprocal_sqrt, bias=BIAS)
+            nc.scalar.activation(inv[t][:], root[t][:], ACT.Square)
 
         out_rows = out_0.rearrange("(p t) j -> p t j", t=PACK)
 
@@ -247,46 +235,56 @@ def tile_picked_tricdmaxbnormbhop_none_po_kernel(
         o_s = sb("o_s", [P, S], U8)
         out_words = out_1[0].rearrange("p n t -> p (n t)").bitcast(I32)
 
-        def planes(h, copy):
-            ob = sb("ob%d" % h, [P, HALF * PACK], BF16)
-            copy(
-                ob[:].rearrange("p (c i t) -> p c t i", t=PACK, i=4),
-                res[:, :, cols(h)].rearrange("p t (c i) -> p c t i", i=4),
-            )
-            o_w = sb("o_w%d" % h, [P, HALF], I32)
-            nc.vector.quantize_mx(o_w[:].bitcast(FP8X4), o_s[:, cols(h)], ob[:])
-            nc.sync.dma_start(out_words[:, cols(h)], o_w[:])
+        for h in range(2):
+            for t in range(PACK):
+                product(qbank[t][:, cols(h)], cd_w, cd_s, t, z_w[h][:], z_s[h][:])
+                nc.scalar.activation(q[t][:, cols(h)], qbank[t][:, cols(h)], ACT.Abs)
+                if h == 1:
+                    nc.sync.dma_start(q_twin[t][:], q[t][:, FRONT])
+        for h in range(2):
+            for t in range(PACK):
+                product(abank[t][:, cols(h)], ca_w, ca_s, t, z_w[h][:], z_s[h][:])
+                copy = nc.vector.tensor_copy if h == 1 and t in (2,3,) else nc.scalar.copy
+                copy(ya[t][:, cols(h)], abank[t][:, cols(h)])
 
-        on_v, on_s = nc.vector.tensor_copy, nc.scalar.copy
-        for h in range(2):
-            for t in range(PACK):
-                q_half(t, h)
-        for h in range(2):
-            for t in range(PACK):
-                a_half(t, h, on_s if t + h <= 3 else on_v)
+        for t in range(2):
+            b_out(t)
         q_sum(0)
         q_sum(1)
-        spread(0, True, on_s)
+        spread(0)
         q_sum(2)
-        spread(1, True, on_s)
+        spread(1)
         q_sum(3)
-        spread(2, True, on_s)
+        b_out(2)
+        spread(2)
+        b_out(3)
+        spread(3)
+
+        def m_fetch(t, c, offsets):
+            fetch(m_other[t][:, c], m_lower[t], offsets)
+            nc.vector.tensor_tensor(num[t][:, c], m_other[t][:, c], m_lower[t][:, c], ALU.subtract)
+
+        def planes(h, copy):
+            o_bf = interleave(copy, "o_bf%d" % h, res[:, :, cols(h)])
+            o_w = sb("o_w%d" % h, [P, HALF], I32)
+            nc.vector.quantize_mx(o_w[:].bitcast(FP8X4), o_s[:, cols(h)], o_bf[:])
+            nc.sync.dma_start(out_words[:, cols(h)], o_w[:])
+
+        inverse(0)
+        inverse(1)
         m_diff(0)
-        spread(3, False, on_s)
-        m_diff(1)
-        inverse(0, FRONT)
         finish(0, FRONT)
-        inverse(1, FRONT)
+        m_diff(1)
         finish(1, FRONT)
-        m_diff(2)
-        inverse(2, FRONT)
-        finish(2, FRONT)
-        inverse(3, FRONT)
+        inverse(2)
+        m_fetch(2, FRONT, l_n5[:])
+        inverse(3)
         for h in range(2):
-            m_diff_scalar(3, h)
+            m_fetch(3, cols(h), entries(l_n5, h))
+            finish(2, cols(h))
             finish(3, cols(h))
-        planes(0, on_s)
-        planes(1, on_v)
+        planes(0, nc.scalar.copy)
+        planes(1, nc.vector.tensor_copy)
         out_scales = out_2[0].bitcast(I32)
-        for quad in range(4):
+        for quad in range(QUADS):
             nc.scalar.dma_start(out_scales[4 * quad : 4 * quad + 4, :], o_s[32 * quad : 32 * quad + 4, :].bitcast(I32))

from contextlib import ExitStack

import concourse.mybir as mybir

T, S, H = 2048, 512, 512
FLOPS = 4 * 2 * 512 * 512 * 512

F32 = mybir.dt.float32
BF16 = mybir.dt.bfloat16
I32 = mybir.dt.int32
U32 = mybir.dt.uint32
U16 = mybir.dt.uint16
U8 = mybir.dt.uint8
FP8X4 = mybir.dt.float8_e4m3fn_x4
ALU = mybir.AluOpType
ACT = mybir.ActivationFunctionType

P = 128
PACK = 4
LAST = PACK - 1
QUADS = 4
PER_COLUMN = 16
LINE_WORDS, LINE_BYTES = 4, 16
HALF = S // 2
PAD = 32
FRONT = slice(0, S)
BACK = slice(S, 2 * S)
BIAS = 8.0


def tile_picked_tricdmaxbnormbhop_none_po_kernel(
    tc, x_words, x_scales, w1_words, w1_scales, gs, offs, n1, n2, ca, cb, cd, n3, n4, n5, n6, out_0, out_1, out_2
):
    nc = tc.nc
    with ExitStack() as ctx:
        keep = ctx.enter_context(tc.tile_pool(name="keep", bufs=1))
        psum = ctx.enter_context(tc.psum_pool(name="psum", bufs=8))

        def sb(name, shape, dtype, reuse=None):
            return keep.tile(shape, dtype, name=name, tag=reuse or name, align_bytes=64)

        def row_tiles(name, width, reuse=None):
            return [sb("%s%d" % (name, t), [P, width], F32, reuse and "%s%d" % (reuse, t)) for t in range(PACK)]

        def load_list(name, dram):
            tile = sb(name, [P, S // PER_COLUMN], U16)
            nc.sync.dma_start(tile[:], dram)
            return tile

        def load_scales(tile, dram, width):
            rows = dram[0].bitcast(I32)
            for quad in range(QUADS):
                src = rows[4 * quad : 4 * quad + 4, :].unsqueeze(0).broadcast_to([8, 4, width // 4])
                nc.sync.dma_start(tile[32 * quad : 32 * quad + 32, :].bitcast(I32), src)

        def cols(h):
            return slice(h * HALF, (h + 1) * HALF)

        def entries(lst, h):
            return lst[:, h * (HALF // PER_COLUMN) : (h + 1) * (HALF // PER_COLUMN)]

        def deal(name, raw, dtype, run, reuse=None):
            dealt = sb(name, [P, S], dtype, reuse)
            nc.vector.tensor_copy(
                dealt[:].rearrange("p (t c i) -> p c t i", t=PACK, i=run),
                raw[:].rearrange("p (c i t) -> p c t i", t=PACK, i=run),
            )
            return dealt

        def deal_words(name, raw):
            return deal(name, raw, I32, LINE_WORDS)

        def deal_bytes(name, raw, reuse=None):
            return deal(name, raw, U8, LINE_BYTES, reuse)

        xs = sb("xs", [P, T], U8)
        load_scales(xs, x_scales, T)
        l_offs = load_list("l_offs", offs)
        l_ca = load_list("l_ca", ca)
        xw = sb("xw", [P, T], I32)
        nc.sync.dma_start(xw[:], x_words[0].rearrange("p n t -> p (n t)").bitcast(I32))
        w1w = sb("w1w", [P, H], I32)
        nc.sync.dma_start(w1w[:], w1_words[0].rearrange("p n t -> p (n t)").bitcast(I32))
        w1s = sb("w1s", [P, H], U8)
        load_scales(w1s, w1_scales, H)
        gain = sb("gain", [P, PACK], F32)
        nc.sync.dma_start(gain[:], gs.rearrange("(p t) o -> p (t o)", t=PACK))
        l_n1 = load_list("l_n1", n1)
        l_cd = load_list("l_cd", cd)
        l_n2 = load_list("l_n2", n2)
        l_cb = load_list("l_cb", cb)
        l_n3 = load_list("l_n3", n3)
        l_n6 = load_list("l_n6", n6)
        l_n4 = load_list("l_n4", n4)
        l_n5 = load_list("l_n5", n5)

        def pick_words(name, lst, reuse=None):
            raw = sb(name, [P, S], I32, reuse)
            nc.vector.tensor_copy(raw[:].bitcast(U32), xw[:].bitcast(U32).indirect(lst[:]))
            return raw

        def pick_bytes(name, lst, reuse=None):
            raw = sb(name, [P, S], U8, reuse)
            nc.vector.tensor_copy(raw[:], xs[:].indirect(lst[:]))
            return raw

        def product(bank, words, scales, t, rhs_words, rhs_scales):
            m = slice(t * P, (t + 1) * P)
            nc.tensor.matmul_mx(
                bank, lhsT=words[:, m].bitcast(FP8X4), lhsT_scale=scales[:, m],
                rhs=rhs_words.bitcast(FP8X4), rhs_scale=rhs_scales, start=True, stop=True,
            )

        def fetch(out, window, offsets):
            nc.scalar.activation(out, window[:].indirect(offsets), ACT.Copy)

        def interleave(copy, name, values):
            rounded = sb(name, [P, HALF * PACK], BF16)
            copy(
                rounded[:].rearrange("p (c i t) -> p c t i", t=PACK, i=LINE_WORDS),
                values.rearrange("p t (c i) -> p c t i", i=LINE_WORDS),
            )
            return rounded

        ya = row_tiles("ya", 2 * S)
        q = row_tiles("q", S + PAD)
        warm = sb("warm", [P, 1], F32)
        nc.gpsimd.memset(warm[:], 1.0)
        warm_out = sb("warm_out", [P, 1], F32)
        nc.scalar.activation(warm_out[:], warm[:], ACT.Abs_reciprocal_sqrt, bias=BIAS)
        for t in range(PACK):
            nc.gpsimd.memset(ya[t][:, BACK], 0.0)
        for t in range(PACK):
            nc.gpsimd.memset(q[t][:, S:], 0.0)

        xq_s = pick_bytes("xq_s", l_offs)
        ca_s_raw = pick_bytes("ca_s_raw", l_ca)
        xq_w = pick_words("xq_w", l_offs)
        w1_w = deal_words("w1_w", w1w)
        w1_s = deal_bytes("w1_s", w1s)
        ca_s = deal_bytes("ca_s", ca_s_raw, "w1w")
        ca_w = deal_words("ca_w", pick_words("ca_w_raw", l_ca, "w1s"))
        cd_s = deal_bytes("cd_s", pick_bytes("cd_s_raw", l_cd))

        y_n1 = row_tiles("y_n1_", S)
        st = row_tiles("st", S)
        st0_twin = sb("st0_twin", [P, S], F32)
        ybank = []
        for t in range(PACK):
            bank = psum.tile([P, S], F32, name="bank")
            product(bank[:], w1_w, w1_s, t, xq_w[:], xq_s[:])
            ybank.append(bank)

        def y_out(t):
            nc.scalar.activation(ya[t][:, FRONT], ybank[t][:], ACT.Copy, scale=gain[:, t : t + 1])

        y_out(0)
        for t in range(PACK):
            if t < LAST:
                y_out(t + 1)
            fetch(y_n1[t][:], ya[t], l_n1[:])
            nc.vector.scalar_tensor_tensor(st[t][:], y_n1[t][:], 0.5, ya[t][:, FRONT], ALU.mult, ALU.add)
            if t == 0:
                nc.vector.tensor_copy(st0_twin[:], st[0][:])
                cd_w = deal_words("cd_w", pick_words("cd_w_raw", l_cd, "y_n1_0"))

        z_w, z_s = [], []
        for h in range(2):
            st_n2 = sb("st_n2_%d" % h, [P, LAST, HALF], F32, "y_n1_%d" % LAST if h else None)
            diff = sb("diff%d" % h, [P, PACK, HALF], F32, "diff")
            nc.vector.tensor_tensor(
                diff[:, 0, :], st[0][:].indirect(entries(l_n2, h)), st0_twin[:, cols(h)], ALU.subtract
            )
            for t in range(1, PACK):
                fetch(st_n2[:, t - 1, :], st[t], entries(l_n2, h))
                nc.vector.tensor_tensor(diff[:, t, :], st_n2[:, t - 1, :], st[t][:, cols(h)], ALU.subtract)
            z_bf = interleave(nc.vector.tensor_copy, "z_bf%d" % h, diff[:])
            words = sb("z_w%d" % h, [P, HALF], I32)
            scales = sb("z_s%d" % h, [P, HALF], U8)
            nc.vector.quantize_mx(words[:].bitcast(FP8X4), scales[:], z_bf[:])
            z_w.append(words)
            z_s.append(scales)

        cb_w_raw = pick_words("cb_w_raw", l_cb, "z_bf1")
        cb_s_raw = pick_bytes("cb_s_raw", l_cb, "diff")
        cb_w = deal_words("cb_w", cb_w_raw)
        cb_s = deal_bytes("cb_s", cb_s_raw)

        b_an3 = row_tiles("b_an3_", 2 * S)
        q_twin = row_tiles("q_twin", S)
        b_n4 = row_tiles("b_n4_", S)
        upper = row_tiles("upper", S)
        m_lower = row_tiles("m_lower", 2 * S, "q_twin")
        m_other = row_tiles("m_other", S)
        num = row_tiles("num", S)
        den = row_tiles("den", S)
        root = row_tiles("root", S)
        inv = row_tiles("inv", S)
        res = sb("res", [P, PACK, S], F32)
        qbank = [psum.tile([P, S], F32, name="bank") for t in range(PACK)]
        abank = [psum.tile([P, S], F32, name="bank") for t in range(PACK)]

        bbank = [psum.tile([P, S], F32, name="bank") for t in range(PACK)]

        def q_sum(t):
            nc.vector.tensor_tensor(den[t][:], q[t][:].indirect(l_n6[:]), q_twin[t][:], ALU.add)

        def b_out(t):
            for h in range(2):
                product(bbank[t][:, cols(h)], cb_w, cb_s, t, z_w[h][:], z_s[h][:])
            (nc.vector.tensor_copy if t in (0,1) else nc.scalar.copy)(b_an3[t][:, FRONT], bbank[t][:])

        def spread(t):
            fetch(b_an3[t][:, BACK], ya[t], l_n3[:])
            nc.vector.tensor_tensor(m_lower[t][:, BACK], bbank[t][:], b_an3[t][:, BACK], ALU.max)
            fetch(b_n4[t][:], b_an3[t], l_n4[:])
            nc.vector.tensor_tensor(upper[t][:], abank[t][:], b_n4[t][:], ALU.min)
            (nc.gpsimd if t in (0,1,2) else nc.vector).tensor_tensor(m_lower[t][:, FRONT], upper[t][:], m_lower[t][:, BACK], ALU.subtract)
            if t < 2:
                nc.sync.dma_start(m_other[t][:], m_lower[t][:, FRONT])

        def m_diff(t):
            nc.vector.tensor_tensor(num[t][:], m_lower[t][:].indirect(l_n5[:]), m_other[t][:], ALU.subtract)

        def inverse(t):
            nc.scalar.activation(root[t][:], den[t][:], ACT.Abs_reciprocal_sqrt, bias=BIAS)
            nc.scalar.activation(inv[t][:], root[t][:], ACT.Square)

        out_rows = out_0.rearrange("(p t) j -> p t j", t=PACK)

        def finish(t, c):
            nc.vector.tensor_tensor(res[:, t, c], num[t][:, c], inv[t][:, c], ALU.mult)
            nc.sync.dma_start(out_rows[:, t, c], res[:, t, c])

        o_s = sb("o_s", [P, S], U8)
        out_words = out_1[0].rearrange("p n t -> p (n t)").bitcast(I32)

        for h in range(2):
            for t in range(PACK):
                product(qbank[t][:, cols(h)], cd_w, cd_s, t, z_w[h][:], z_s[h][:])
                nc.scalar.activation(q[t][:, cols(h)], qbank[t][:, cols(h)], ACT.Abs)
                if h == 1:
                    nc.sync.dma_start(q_twin[t][:], q[t][:, FRONT])
        for h in range(2):
            for t in range(PACK):
                product(abank[t][:, cols(h)], ca_w, ca_s, t, z_w[h][:], z_s[h][:])
                copy = nc.vector.tensor_copy if h == 1 and t in (2,3,) else nc.scalar.copy
                copy(ya[t][:, cols(h)], abank[t][:, cols(h)])

        for t in range(2):
            b_out(t)
        q_sum(0)
        q_sum(1)
        spread(0)
        q_sum(2)
        spread(1)
        q_sum(3)
        b_out(2)
        spread(2)
        b_out(3)
        spread(3)

        def m_fetch(t, c, offsets):
            fetch(m_other[t][:, c], m_lower[t], offsets)
            nc.vector.tensor_tensor(num[t][:, c], m_other[t][:, c], m_lower[t][:, c], ALU.subtract)

        def planes(h, copy):
            o_bf = interleave(copy, "o_bf%d" % h, res[:, :, cols(h)])
            o_w = sb("o_w%d" % h, [P, HALF], I32)
            nc.vector.quantize_mx(o_w[:].bitcast(FP8X4), o_s[:, cols(h)], o_bf[:])
            nc.sync.dma_start(out_words[:, cols(h)], o_w[:])

        inverse(0)
        inverse(1)
        m_diff(0)
        finish(0, FRONT)
        m_diff(1)
        finish(1, FRONT)
        inverse(2)
        m_fetch(2, FRONT, l_n5[:])
        inverse(3)
        for h in range(2):
            m_fetch(3, cols(h), entries(l_n5, h))
            finish(2, cols(h))
            finish(3, cols(h))
        planes(0, nc.scalar.copy)
        planes(1, nc.vector.tensor_copy)
        out_scales = out_2[0].bitcast(I32)
        for quad in range(QUADS):
            nc.scalar.dma_start(out_scales[4 * quad : 4 * quad + 4, :], o_s[32 * quad : 32 * quad + 4, :].bitcast(I32))
